import numpy as np
import ml_dtypes


def mxq(x, axis, fmt="e4m3"):
    dtype, down = {"e4m3": (ml_dtypes.float8_e4m3fn, 7), "e5m2": (ml_dtypes.float8_e5m2, 14)}[fmt]
    v = np.moveaxis(np.asarray(x, np.float32).astype(ml_dtypes.bfloat16).astype(np.float64), axis, -1)
    blocks = v.reshape(v.shape[:-1] + (-1, 32))
    amax = np.abs(blocks).max(-1, keepdims=True)
    byte = np.maximum(np.where(amax > 0, np.frexp(amax)[1] - 1 + 127, 0) - down, 1)
    scale = np.exp2(byte - 127.0)
    codes = (blocks / scale).astype(np.float32).astype(dtype).astype(np.float64)
    return np.moveaxis((codes * scale).reshape(v.shape), -1, axis)


WIDE = False


def mx_kscale(k):
    if not WIDE:
        return np.ones(k)
    levels = np.array([10, -10, 5, -5, 0])
    if k % 512:
        return np.exp2(np.random.permutation(np.resize(levels, k // 32))).repeat(32)
    a = np.empty((k // 512, 16))
    for p in range(k // 512):
        a[p, :8] = np.random.permutation(np.resize(levels, 8))
        for g in range(8):
            far = levels[np.abs(levels - a[p, g]) >= 10]
            a[p, g + 8] = far[np.random.randint(len(far))]
    return np.exp2(a.ravel()).repeat(32)


def f64(x):
    return np.asarray(x).astype(np.float64)


def striped(idx):
    return np.tile(idx.reshape(-1, 16).T, (8, 1)).astype(np.uint16)


def unstriped(offs):
    return offs[:16].T.reshape(-1).astype(np.int64)


E2M1 = np.array([0.0, 0.5, 1.0, 1.5, 2.0, 3.0, 4.0, 6.0, -0.0, -0.5, -1.0, -1.5, -2.0, -3.0, -4.0, -6.0])


def pack_weight(w, fmt):
    k, n = w.shape
    w = f64(np.asarray(w, np.float32).astype(ml_dtypes.bfloat16)).reshape(k // 32, 32, n)
    amax = np.abs(w).max(1)
    if fmt == "e4m3":
        byte = np.frexp(amax)[1] - 1 + 127 - 7
    else:
        mant, ex = np.frexp(amax / 6.0)
        byte = np.where(mant > 0.5, ex, ex - 1) + 127
    byte = np.clip(np.where(amax > 0, byte, 1), 1, 254)
    scaled = (w * np.exp2(127.0 - byte)[:, None, :]).reshape(k, n).astype(np.float32)
    by_word = np.ascontiguousarray(scaled.reshape(k // 512, 128, 4, n).transpose(0, 1, 3, 2))
    if fmt == "e4m3":
        words = by_word.astype(ml_dtypes.float8_e4m3fn).view(np.uint8)
    else:
        c = by_word.astype(ml_dtypes.float4_e2m1fn).view(np.uint8) & 0xF
        words = (c[..., 0::2] | (c[..., 1::2] << 4)).reshape(k // 512, 128, 2 * n)
    return np.ascontiguousarray(words), np.ascontiguousarray(byte.astype(np.uint8).reshape(k // 512, 16, n))


def unpack_weight(words, scales, fmt):
    g, _, n = scales.shape
    words = np.ascontiguousarray(words).reshape(g, 128, n, -1)
    if fmt == "e4m3":
        vals = words.view(ml_dtypes.float8_e4m3fn).astype(np.float64)
    else:
        nib = np.empty((g, 128, n, 4), np.uint8)
        nib[..., 0::2] = words & 0xF
        nib[..., 1::2] = words >> 4
        vals = E2M1[nib]
    vals = vals * np.repeat(np.exp2(scales.astype(np.float64) - 127.0), 8, axis=1)[..., None]
    return vals.transpose(0, 1, 3, 2).reshape(g * 512, n)


def gelu(v):
    return 0.5 * v * (1.0 + np.tanh(np.sqrt(2.0 / np.pi) * (v + 0.044715 * v**3)))


K, T, S, H, T3, S2, P = 1024, 4096, 1024, 1024, 2048, 512, 512


def setup_inputs():
    n = np.random.standard_normal
    s = mx_kscale(K)[:, None]
    u = mx_kscale(H)[:, None]
    d = {}
    d["tab_words"], d["tab_scales"] = pack_weight(n((K, T)) * s, "e4m3")
    d["offs"] = striped(np.random.permutation(T)[:S])
    d["tab2_words"], d["tab2_scales"] = pack_weight(n((H, T3)) / u / H ** 0.5, "e4m3")
    d["offs2"] = striped(np.random.permutation(T3)[:S2])
    d["pos1"] = striped(np.random.permutation(S)[:P])
    d["pos2"] = striped(np.random.permutation(S)[:P])
    d["w1"] = (n((K, H)) / s * u.T / K ** 0.5).astype(np.float32)
    d["w2_words"], d["w2_scales"] = pack_weight(1.6 * n((K, H)) / s / K ** 0.5, "e2m1")
    d["dens"] = (np.exp(0.5 * n((H, S))) * u).astype(np.float32)
    d["sharp"] = (1.2 * np.exp(0.4 * n(S2))).astype(np.float32)
    return d


def reference(tab_words, tab_scales, offs, tab2_words, tab2_scales, offs2,
              pos1, pos2, w1, w2_words, w2_scales, dens, sharp):
    v = unpack_weight(tab_words, tab_scales, "e4m3")[:, unstriped(offs)]
    v2 = unpack_weight(tab2_words, tab2_scales, "e4m3")[:, unstriped(offs2)]
    w1q = mxq(f64(w1), 0, "e4m3")
    w2 = unpack_weight(w2_words, w2_scales, "e2m1")
    texture = np.tanh(w2.T @ v)
    h = (w1q.T @ v) + texture * f64(dens)
    hq = mxq(h, 0, "e4m3")
    e = v2.T @ hq
    root = e[:, unstriped(pos1)]
    cap = e[:, unstriped(pos2)]
    weight = 1.0 / (1.0 + np.exp(-(root * f64(sharp)[:, None])))
    return (root - cap) * weight

@@ -1,0 +1,306 @@
+from contextlib import ExitStack
+
+import concourse.mybir as mybir
+
+K, T, S, H, T3, S2, NP = 1024, 4096, 1024, 1024, 2048, 512, 512
+FLOPS = 2 * (2 * K * H * S + H * S2 * S)
+
+F32 = mybir.dt.float32
+BF16 = mybir.dt.bfloat16
+I32 = mybir.dt.int32
+U32 = mybir.dt.uint32
+U16 = mybir.dt.uint16
+U8 = mybir.dt.uint8
+FP8X4 = mybir.dt.float8_e4m3fn_x4
+FP4X4 = mybir.dt.float4_e2m1fn_x4
+ALU = mybir.AluOpType
+ACT = mybir.ActivationFunctionType
+
+P = 128
+HALF = 512
+
+
+def tile_list_weld_pass_scores_kernel(
+    tc, tab_words, tab_scales, offs, tab2_words, tab2_scales, offs2, pos1, pos2, w1, w2_words, w2_scales, dens, sharp, out
+):
+    nc = tc.nc
+    with ExitStack() as ctx:
+        lists = ctx.enter_context(tc.tile_pool(name="lists", bufs=1))
+        keep = ctx.enter_context(tc.tile_pool(name="keep", bufs=1))
+        ring = ctx.enter_context(tc.tile_pool(name="ring", bufs=2))
+        psum = ctx.enter_context(tc.psum_pool(name="psum", bufs=1))
+
+        def held(shape, dtype, name, tag=""):
+            return keep.tile(shape, dtype, name=name, tag=tag, align_bytes=64)
+
+        offs_sb = lists.tile([P, S // 16], U16, name="offs_sb")
+        offs2_sb = lists.tile([P, S2 // 16], U16, name="offs2_sb")
+        pos1_sb = lists.tile([P, NP // 16], U16, name="pos1_sb")
+        pos2_sb = lists.tile([P, NP // 16], U16, name="pos2_sb")
+
+        tab_s = held([P, 2, T], U8, "tab_s")
+        w2_s = held([P, 2, H], U8, "w2_s")
+        tab2_s = held([P, T3], U8, "tab2_s")
+        w2_w = held([P, 2, 2 * H], U8, "w2_w")
+        tab_w = [held([P, T], I32, "tab_w%d" % a) for a in range(2)]
+        tab2_w = [held([P, T3], I32, "tab2_w%d" % a) for a in range(2)]
+        sharp_sb = held([P, 4], F32, "sharp_sb")
+
+        nc.vector.memset(tab_s[:].rearrange("p a t -> p (a t)").bitcast(I32), 0)
+        nc.gpsimd.memset(w2_s[:].rearrange("p a t -> p (a t)").bitcast(I32), 0)
+        nc.gpsimd.memset(tab2_s[:].bitcast(I32), 0)
+
+        nc.sync.dma_start(offs_sb[:], offs)
+        nc.sync.dma_start(w2_w[:].bitcast(I32), w2_words.rearrange("a p c -> p a c").bitcast(I32))
+        for q in range(4):
+            nc.sync.dma_start(
+                tab_s[32 * q : 32 * q + 4, :, :].bitcast(I32),
+                tab_scales[:, 4 * q : 4 * q + 4, :].rearrange("a r t -> r a t").bitcast(I32),
+            )
+        for q in range(4):
+            nc.gpsimd.dma_start(
+                w2_s[32 * q : 32 * q + 4, :, :].bitcast(I32),
+                w2_scales[:, 4 * q : 4 * q + 4, :].rearrange("a r t -> r a t").bitcast(I32),
+            )
+        for q in range(4):
+            nc.gpsimd.dma_start(
+                tab2_s[32 * q : 32 * q + 8, :].bitcast(I32),
+                tab2_scales[:, 4 * q : 4 * q + 4, :].bitcast(I32),
+            )
+        for a in range(2):
+            nc.sync.dma_start(tab_w[a][:], tab_words[a].rearrange("p t i -> p (t i)").bitcast(I32))
+
+        dens_sb = {}
+        w1_raw = {}
+
+        def load_dens(b, jh):
+            dens_sb[b, jh] = held([P, 4, HALF], F32, "dens%d%d" % (b, jh))
+            nc.sync.dma_start(
+                dens_sb[b, jh][:],
+                dens[512 * b : 512 * (b + 1), HALF * jh : HALF * (jh + 1)].rearrange("(p t) j -> p t j", t=4),
+            )
+
+        def load_w1(a, b):
+            w1_raw[a, b] = held([P, 4, 512], F32, "w1_raw%d%d" % (a, b), tag="slot%d%d" % (a, b))
+            nc.sync.dma_start(
+                w1_raw[a, b][:],
+                w1[512 * a : 512 * (a + 1), 512 * b : 512 * (b + 1)].rearrange("(p i) c -> p i c", i=4),
+            )
+
+        load_dens(0, 0)
+        load_w1(0, 0)
+        load_w1(1, 0)
+        load_dens(0, 1)
+        load_w1(0, 1)
+        load_w1(1, 1)
+        load_dens(1, 0)
+        nc.sync.dma_start(offs2_sb[:], offs2)
+        for a in range(2):
+            nc.sync.dma_start(tab2_w[a][:], tab2_words[a].rearrange("p t i -> p (t i)").bitcast(I32))
+        load_dens(1, 1)
+        nc.sync.dma_start(pos1_sb[:], pos1)
+        nc.sync.dma_start(pos2_sb[:], pos2)
+        with nc.allow_non_contiguous_dma("one factor a partition"):
+            nc.sync.dma_start(sharp_sb[:], sharp.rearrange("(c p) -> p c", p=P))
+
+        w2_c = held([P, 2, 2 * H], U8, "w2_c")
+        w2_p = held([P, 2, H], U8, "w2_p")
+        nc.vector.tensor_copy(
+            w2_c[:].rearrange("p a c -> p (a c)").bitcast(U16).rearrange("p (g t m) -> p g t m", t=4, m=P),
+            w2_w[:].rearrange("p a c -> p (a c)").bitcast(U16).rearrange("p (g m t) -> p g t m", t=4, m=P),
+        )
+
+        v_w, v_s = {}, {}
+
+        def gather_v_words(a, jh):
+            v_w[a, jh] = held([P, HALF], U32, "v_w%d%d" % (a, jh))
+            nc.vector.tensor_copy(v_w[a, jh][:], tab_w[a][:].bitcast(U32).indirect(offs_sb[:, 32 * jh : 32 * (jh + 1)]))
+
+        def gather_v_scales(a, jh):
+            v_s[a, jh] = held([P, HALF], U8, "v_s%d%d" % (a, jh))
+            nc.vector.tensor_copy(v_s[a, jh][:], tab_s[:, a, :].indirect(offs_sb[:, 32 * jh : 32 * (jh + 1)]))
+
+        for jh in range(2):
+            gather_v_scales(0, jh)
+        for jh in range(2):
+            gather_v_words(0, jh)
+        nc.vector.tensor_copy(
+            w2_p[:].rearrange("p a (b t m) -> p (a b) t m", t=4, m=P),
+            w2_s[:].rearrange("p a (b m t) -> p (a b) t m", t=4, m=P),
+        )
+        for jh in range(2):
+            gather_v_scales(1, jh)
+        for jh in range(2):
+            gather_v_words(1, jh)
+
+        w1_bf, w1_c, w1_s = {}, {}, {}
+
+        def cast_w1(a, b, copy):
+            w1_bf[a, b] = ring.tile([P, 4, P, 4], BF16, name="w1_bf", align_bytes=64)
+            copy(
+                w1_bf[a, b][:].rearrange("p t m i -> p m i t"),
+                w1_raw[a, b][:].rearrange("p i (m t) -> p m i t", t=4),
+            )
+
+        def quant_w1(a, b):
+            w1_c[a, b] = held([P, 512], U32, "w1_c%d%d" % (a, b))
+            w1_s[a, b] = held([P, 512], U8, "w1_s%d%d" % (a, b))
+            nc.vector.quantize_mx(
+                out=w1_c[a, b][:].bitcast(FP8X4),
+                scales=w1_s[a, b][:],
+                in_=w1_bf[a, b][:].rearrange("p t m i -> p (t m i)"),
+            )
+
+        tex, lin, h_bf, h_c, h_s = {}, {}, {}, {}, {}
+
+        def texture(b, jh):
+            tex[b, jh] = ring.tile([P, 4, HALF], F32, name="tex")
+            for t in range(4):
+                bank = psum.tile([P, HALF], F32, name="tex_bank", bufs=3)
+                c0 = 512 * b + P * t
+                for a in range(2):
+                    nc.tensor.matmul_mx(
+                        out=bank[:],
+                        lhsT=w2_c[:, a, 2 * c0 : 2 * (c0 + P)].bitcast(FP4X4),
+                        lhsT_scale=w2_p[:, a, c0 : c0 + P],
+                        rhs=v_w[a, jh][:].bitcast(FP8X4),
+                        rhs_scale=v_s[a, jh][:],
+                        start=(a == 0),
+                        stop=(a == 1),
+                    )
+                nc.scalar.activation(tex[b, jh][:, t, :], bank[:], ACT.Tanh)
+
+        def weigh(b, jh, t):
+            nc.vector.tensor_tensor(tex[b, jh][:, t, :], tex[b, jh][:, t, :], dens_sb[b, jh][:, t, :], ALU.mult)
+
+        def linear(b, jh, u):
+            lin[b, jh, u] = psum.tile([P, 4, P], F32, name="lin_bank", bufs=3)
+            cols = slice(P * u, P * (u + 1))
+            for t in range(4):
+                for a in range(2):
+                    nc.tensor.matmul_mx(
+                        out=lin[b, jh, u][:, t, :],
+                        lhsT=w1_c[a, b][:, P * t : P * (t + 1)].bitcast(FP8X4),
+                        lhsT_scale=w1_s[a, b][:, P * t : P * (t + 1)],
+                        rhs=v_w[a, jh][:, cols].bitcast(FP8X4),
+                        rhs_scale=v_s[a, jh][:, cols],
+                        start=(a == 0),
+                        stop=(a == 1),
+                    )
+
+        def combine(b, jh, u):
+            if u == 0:
+                h_bf[b, jh] = ring.tile([P, HALF, 4], BF16, name="h_bf", align_bytes=64)
+            cols = slice(P * u, P * (u + 1))
+            nc.vector.tensor_tensor(
+                h_bf[b, jh][:, cols, :].rearrange("p (c i) t -> p c t i", i=2),
+                lin[b, jh, u][:].rearrange("p t (c i) -> p c t i", i=2),
+                tex[b, jh][:, :, cols].rearrange("p t (c i) -> p c t i", i=2),
+                ALU.add,
+            )
+
+        def quant_h(b, jh):
+            h_c[b, jh] = held([P, HALF], U32, "h_c%d%d" % (b, jh))
+            h_s[b, jh] = held([P, HALF], U8, "h_s%d%d" % (b, jh))
+            nc.vector.quantize_mx(
+                out=h_c[b, jh][:].bitcast(FP8X4),
+                scales=h_s[b, jh][:],
+                in_=h_bf[b, jh][:].rearrange("p j t -> p (j t)"),
+            )
+
+        v2_w, v2_s = {}, {}
+
+        def gather_v2(mh):
+            sl = offs2_sb[:, 16 * mh : 16 * (mh + 1)]
+            v2_s[mh] = held([P, 256], U8, "v2_s%d" % mh)
+            nc.vector.tensor_copy(v2_s[mh][:], tab2_s[:].indirect(sl))
+            for a in range(2):
+                v2_w[a, mh] = held([P, 256], U32, "v2_w%d%d" % (a, mh))
+                nc.vector.tensor_copy(v2_w[a, mh][:], tab2_w[a][:].bitcast(U32).indirect(sl))
+
+        e_sb = {}
+
+        def scores(mt, jh):
+            if jh == 0:
+                e_sb[mt] = held([P, S], F32, "e%d" % mt, tag="slot%d%d" % (mt % 2, mt // 2))
+            bank = psum.tile([P, HALF], F32, name="e_bank", bufs=2)
+            cols = slice(P * (mt % 2), P * (mt % 2 + 1))
+            for b in range(2):
+                nc.tensor.matmul_mx(
+                    out=bank[:],
+                    lhsT=v2_w[b, mt // 2][:, cols].bitcast(FP8X4),
+                    lhsT_scale=v2_s[mt // 2][4 * b :, cols],
+                    rhs=h_c[b, jh][:].bitcast(FP8X4),
+                    rhs_scale=h_s[b, jh][:],
+                    start=(b == 0),
+                    stop=(b == 1),
+                )
+            nc.scalar.copy(e_sb[mt][:, HALF * jh : HALF * (jh + 1)], bank[:])
+
+        def chunk(b, jh, before_combine):
+            for t in range(4):
+                weigh(b, jh, t)
+            before_combine()
+            for u in range(4):
+                linear(b, jh, u)
+                combine(b, jh, u)
+
+        def w1_first():
+            for a in range(2):
+                cast_w1(a, 0, nc.vector.tensor_copy)
+            for a in range(2):
+                quant_w1(a, 0)
+
+        texture(0, 0)
+        texture(0, 1)
+        chunk(0, 0, w1_first)
+        for a in range(2):
+            cast_w1(a, 1, nc.scalar.copy)
+        texture(1, 0)
+        chunk(0, 1, lambda: quant_h(0, 0))
+        for a in range(2):
+            quant_w1(a, 1)
+        texture(1, 1)
+        chunk(1, 0, lambda: quant_h(0, 1))
+        gather_v2(0)
+        quant_h(1, 0)
+        scores(0, 0)
+        scores(1, 0)
+        chunk(1, 1, lambda: None)
+        quant_h(1, 1)
+        gather_v2(1)
+        scores(0, 1)
+        scores(1, 1)
+        for mt in (2, 3):
+            for jh in range(2):
+                scores(mt, jh)
+
+        root, diff, wgt = {}, {}, {}
+
+        def pick_root(mt):
+            root[mt] = ring.tile([P, NP], F32, name="root", bufs=4)
+            nc.vector.tensor_copy(root[mt][:], e_sb[mt][:].indirect(pos1_sb[:]))
+            wgt[mt] = ring.tile([P, NP], F32, name="wgt", bufs=3)
+            nc.scalar.activation(wgt[mt][:], root[mt][:], ACT.Sigmoid, scale=sharp_sb[:, mt : mt + 1])
+
+        def pick_cap(mt):
+            diff[mt] = ring.tile([P, NP], F32, name="diff")
+            nc.vector.tensor_tensor(diff[mt][:], e_sb[mt][:].indirect(pos2_sb[:]), root[mt][:], ALU.subtract)
+
+        def finish(mt):
+            res = ring.tile([P, NP], F32, name="res", bufs=4)
+            nc.vector.scalar_tensor_tensor(res[:], diff[mt][:], -1.0, wgt[mt][:], ALU.mult, ALU.mult)
+            nc.sync.dma_start(out[P * mt : P * (mt + 1), :], res[:])
+
+        pick_root(0)
+        pick_root(1)
+        pick_cap(0)
+        pick_root(2)
+        finish(0)
+        pick_cap(1)
+        pick_root(3)
+        finish(1)
+        pick_cap(2)
+        pick_cap(3)
+        finish(2)
+        finish(3)

@@ -46,29 +46,31 @@ def tile_list_weld_pass_scores_kernel(
         tab2_w = [held([P, T3], I32, "tab2_w%d" % a) for a in range(2)]
         sharp_sb = held([P, 4], F32, "sharp_sb")
 
-        nc.vector.memset(tab_s[:].rearrange("p a t -> p (a t)").bitcast(I32), 0)
-        nc.gpsimd.memset(w2_s[:].rearrange("p a t -> p (a t)").bitcast(I32), 0)
+        nc.gpsimd.memset(tab_s[:, 0, :].bitcast(I32), 0)
+        nc.vector.memset(tab_s[:, 1, :].bitcast(I32), 0)
+        nc.vector.memset(w2_s[:].rearrange("p a t -> p (a t)").bitcast(I32), 0)
         nc.gpsimd.memset(tab2_s[:].bitcast(I32), 0)
 
         nc.sync.dma_start(offs_sb[:], offs)
+        nc.sync.dma_start(offs2_sb[:], offs2)
+        nc.sync.dma_start(pos1_sb[:], pos1)
+        nc.sync.dma_start(pos2_sb[:], pos2)
         nc.sync.dma_start(w2_w[:].bitcast(I32), w2_words.rearrange("a p c -> p a c").bitcast(I32))
-        for q in range(4):
+        for q in (0, 2, 1, 3):
             nc.sync.dma_start(
                 tab_s[32 * q : 32 * q + 4, :, :].bitcast(I32),
                 tab_scales[:, 4 * q : 4 * q + 4, :].rearrange("a r t -> r a t").bitcast(I32),
             )
-        for q in range(4):
-            nc.gpsimd.dma_start(
+
+        def load_tab(a):
+            nc.sync.dma_start(tab_w[a][:], tab_words[a].rearrange("p t i -> p (t i)").bitcast(I32))
+
+        load_tab(0)
+        for q in (0, 2, 1, 3):
+            nc.sync.dma_start(
                 w2_s[32 * q : 32 * q + 4, :, :].bitcast(I32),
                 w2_scales[:, 4 * q : 4 * q + 4, :].rearrange("a r t -> r a t").bitcast(I32),
             )
-        for q in range(4):
-            nc.gpsimd.dma_start(
-                tab2_s[32 * q : 32 * q + 8, :].bitcast(I32),
-                tab2_scales[:, 4 * q : 4 * q + 4, :].bitcast(I32),
-            )
-        for a in range(2):
-            nc.sync.dma_start(tab_w[a][:], tab_words[a].rearrange("p t i -> p (t i)").bitcast(I32))
 
         dens_sb = {}
         w1_raw = {}
@@ -87,19 +89,22 @@ def tile_list_weld_pass_scores_kernel(
                 w1[512 * a : 512 * (a + 1), 512 * b : 512 * (b + 1)].rearrange("(p i) c -> p i c", i=4),
             )
 
-        load_dens(0, 0)
         load_w1(0, 0)
         load_w1(1, 0)
+        load_tab(1)
+        load_dens(0, 0)
         load_dens(0, 1)
         load_w1(0, 1)
         load_w1(1, 1)
         load_dens(1, 0)
-        nc.sync.dma_start(offs2_sb[:], offs2)
+        load_dens(1, 1)
+        for q in (0, 2, 1, 3):
+            nc.sync.dma_start(
+                tab2_s[32 * q : 32 * q + 8, :].bitcast(I32),
+                tab2_scales[:, 4 * q : 4 * q + 4, :].bitcast(I32),
+            )
         for a in range(2):
             nc.sync.dma_start(tab2_w[a][:], tab2_words[a].rearrange("p t i -> p (t i)").bitcast(I32))
-        load_dens(1, 1)
-        nc.sync.dma_start(pos1_sb[:], pos1)
-        nc.sync.dma_start(pos2_sb[:], pos2)
         with nc.allow_non_contiguous_dma("one factor a partition"):
             nc.sync.dma_start(sharp_sb[:], sharp.rearrange("(c p) -> p c", p=P))
 
@@ -112,35 +117,26 @@ def tile_list_weld_pass_scores_kernel(
 
         v_w, v_s = {}, {}
 
-        def gather_v_words(a, jh):
-            v_w[a, jh] = held([P, HALF], U32, "v_w%d%d" % (a, jh))
-            nc.vector.tensor_copy(v_w[a, jh][:], tab_w[a][:].bitcast(U32).indirect(offs_sb[:, 32 * jh : 32 * (jh + 1)]))
+        for a in range(2):
+            v_w[a] = held([P, S], U32, "v_w%d" % a)
+            v_s[a] = held([P, S], U8, "v_s%d" % a)
 
-        def gather_v_scales(a, jh):
-            v_s[a, jh] = held([P, HALF], U8, "v_s%d%d" % (a, jh))
-            nc.vector.tensor_copy(v_s[a, jh][:], tab_s[:, a, :].indirect(offs_sb[:, 32 * jh : 32 * (jh + 1)]))
+        def gather_v_words(a, j0, j1):
+            nc.vector.tensor_copy(v_w[a][:, j0:j1], tab_w[a][:].bitcast(U32).indirect(offs_sb[:, j0 // 16 : j1 // 16]))
 
-        for jh in range(2):
-            gather_v_scales(0, jh)
-        for jh in range(2):
-            gather_v_words(0, jh)
-        nc.vector.tensor_copy(
-            w2_p[:].rearrange("p a (b t m) -> p (a b) t m", t=4, m=P),
-            w2_s[:].rearrange("p a (b m t) -> p (a b) t m", t=4, m=P),
-        )
-        for jh in range(2):
-            gather_v_scales(1, jh)
-        for jh in range(2):
-            gather_v_words(1, jh)
+        def gather_v_scales(a):
+            nc.vector.tensor_copy(v_s[a][:], tab_s[:, a, :].indirect(offs_sb[:]))
 
         w1_bf, w1_c, w1_s = {}, {}, {}
 
-        def cast_w1(a, b, copy):
+        def cast_w1(a, b, copy, parts):
             w1_bf[a, b] = ring.tile([P, 4, P, 4], BF16, name="w1_bf", align_bytes=64)
-            copy(
-                w1_bf[a, b][:].rearrange("p t m i -> p m i t"),
-                w1_raw[a, b][:].rearrange("p i (m t) -> p m i t", t=4),
-            )
+            for m0 in range(0, P, P // parts):
+                ms = slice(m0, m0 + P // parts)
+                copy(
+                    w1_bf[a, b][:].rearrange("p t m i -> p m t i")[:, ms],
+                    w1_raw[a, b][:].rearrange("p i (m t) -> p m t i", t=4)[:, ms],
+                )
 
         def quant_w1(a, b):
             w1_c[a, b] = held([P, 512], U32, "w1_c%d%d" % (a, b))
@@ -163,27 +159,27 @@ def tile_list_weld_pass_scores_kernel(
                         out=bank[:],
                         lhsT=w2_c[:, a, 2 * c0 : 2 * (c0 + P)].bitcast(FP4X4),
                         lhsT_scale=w2_p[:, a, c0 : c0 + P],
-                        rhs=v_w[a, jh][:].bitcast(FP8X4),
-                        rhs_scale=v_s[a, jh][:],
+                        rhs=v_w[a][:, HALF * jh : HALF * (jh + 1)].bitcast(FP8X4),
+                        rhs_scale=v_s[a][:, HALF * jh : HALF * (jh + 1)],
                         start=(a == 0),
                         stop=(a == 1),
                     )
                 nc.scalar.activation(tex[b, jh][:, t, :], bank[:], ACT.Tanh)
 
-        def weigh(b, jh, t):
-            nc.vector.tensor_tensor(tex[b, jh][:, t, :], tex[b, jh][:, t, :], dens_sb[b, jh][:, t, :], ALU.mult)
+        def weigh(b, jh, ts):
+            nc.vector.tensor_tensor(tex[b, jh][:, ts, :], tex[b, jh][:, ts, :], dens_sb[b, jh][:, ts, :], ALU.mult)
 
         def linear(b, jh, u):
             lin[b, jh, u] = psum.tile([P, 4, P], F32, name="lin_bank", bufs=3)
-            cols = slice(P * u, P * (u + 1))
+            cols = slice(HALF * jh + P * u, HALF * jh + P * (u + 1))
             for t in range(4):
                 for a in range(2):
                     nc.tensor.matmul_mx(
                         out=lin[b, jh, u][:, t, :],
                         lhsT=w1_c[a, b][:, P * t : P * (t + 1)].bitcast(FP8X4),
                         lhsT_scale=w1_s[a, b][:, P * t : P * (t + 1)],
-                        rhs=v_w[a, jh][:, cols].bitcast(FP8X4),
-                        rhs_scale=v_s[a, jh][:, cols],
+                        rhs=v_w[a][:, cols].bitcast(FP8X4),
+                        rhs_scale=v_s[a][:, cols],
                         start=(a == 0),
                         stop=(a == 1),
                     )
@@ -210,13 +206,15 @@ def tile_list_weld_pass_scores_kernel(
 
         v2_w, v2_s = {}, {}
 
-        def gather_v2(mh):
-            sl = offs2_sb[:, 16 * mh : 16 * (mh + 1)]
+        def gather_v2_scales(mh):
             v2_s[mh] = held([P, 256], U8, "v2_s%d" % mh)
-            nc.vector.tensor_copy(v2_s[mh][:], tab2_s[:].indirect(sl))
-            for a in range(2):
-                v2_w[a, mh] = held([P, 256], U32, "v2_w%d%d" % (a, mh))
-                nc.vector.tensor_copy(v2_w[a, mh][:], tab2_w[a][:].bitcast(U32).indirect(sl))
+            nc.vector.tensor_copy(v2_s[mh][:], tab2_s[:].indirect(offs2_sb[:, 16 * mh : 16 * (mh + 1)]))
+
+        def gather_v2_words(a, mh):
+            v2_w[a, mh] = held([P, 256], U32, "v2_w%d%d" % (a, mh))
+            nc.vector.tensor_copy(
+                v2_w[a, mh][:], tab2_w[a][:].bitcast(U32).indirect(offs2_sb[:, 16 * mh : 16 * (mh + 1)])
+            )
 
         e_sb = {}
 
@@ -237,41 +235,54 @@ def tile_list_weld_pass_scores_kernel(
                 )
             nc.scalar.copy(e_sb[mt][:, HALF * jh : HALF * (jh + 1)], bank[:])
 
-        def chunk(b, jh, before_combine):
-            for t in range(4):
-                weigh(b, jh, t)
+        def chunk(b, jh, step, before_combine):
+            for t in range(0, 4, step):
+                weigh(b, jh, slice(t, t + step))
             before_combine()
             for u in range(4):
                 linear(b, jh, u)
                 combine(b, jh, u)
 
-        def w1_first():
-            for a in range(2):
-                cast_w1(a, 0, nc.vector.tensor_copy)
-            for a in range(2):
-                quant_w1(a, 0)
+        for a in range(2):
+            gather_v_scales(a)
+        gather_v_words(0, 0, S)
+        nc.vector.tensor_copy(
+            w2_p[:].rearrange("p a (b t m) -> p (a b) t m", t=4, m=P),
+            w2_s[:].rearrange("p a (b m t) -> p (a b) t m", t=4, m=P),
+        )
+        for a in range(2):
+            cast_w1(a, 0, nc.vector.tensor_copy, 1)
+        for a in range(2):
+            quant_w1(a, 0)
+        for jh in range(2):
+            gather_v_words(1, HALF * jh, HALF * (jh + 1))
 
         texture(0, 0)
         texture(0, 1)
-        chunk(0, 0, w1_first)
-        for a in range(2):
-            cast_w1(a, 1, nc.scalar.copy)
+        chunk(0, 0, 1, lambda: None)
         texture(1, 0)
-        chunk(0, 1, lambda: quant_h(0, 0))
         for a in range(2):
-            quant_w1(a, 1)
+            cast_w1(a, 1, nc.scalar.copy, 2)
+        chunk(0, 1, 4, lambda: quant_h(0, 0))
         texture(1, 1)
-        chunk(1, 0, lambda: quant_h(0, 1))
-        gather_v2(0)
-        quant_h(1, 0)
-        scores(0, 0)
-        scores(1, 0)
-        chunk(1, 1, lambda: None)
+
+        def before_third():
+            quant_h(0, 1)
+            for a in range(2):
+                quant_w1(a, 1)
+
+        chunk(1, 0, 4, before_third)
+        chunk(1, 1, 4, lambda: quant_h(1, 0))
+        gather_v2_scales(0)
+        for a in range(2):
+            gather_v2_words(a, 0)
         quant_h(1, 1)
-        gather_v2(1)
+        gather_v2_scales(1)
+        for a in range(2):
+            gather_v2_words(a, 1)
+        scores(0, 0)
         scores(0, 1)
-        scores(1, 1)
-        for mt in (2, 3):
+        for mt in (1, 2, 3):
             for jh in range(2):
                 scores(mt, jh)
 

@@ -75,12 +75,11 @@ def tile_list_weld_pass_scores_kernel(
         dens_sb = {}
         w1_raw = {}
 
-        def load_dens(b, jh):
+        def load_dens(b, jh, step=4):
             dens_sb[b, jh] = held([P, 4, HALF], F32, "dens%d%d" % (b, jh))
-            nc.sync.dma_start(
-                dens_sb[b, jh][:],
-                dens[512 * b : 512 * (b + 1), HALF * jh : HALF * (jh + 1)].rearrange("(p t) j -> p t j", t=4),
-            )
+            rows = dens[512 * b : 512 * (b + 1), HALF * jh : HALF * (jh + 1)].rearrange("(p t) j -> p t j", t=4)
+            for t in range(0, 4, step):
+                nc.sync.dma_start(dens_sb[b, jh][:, t : t + step, :], rows[:, t : t + step, :])
 
         def load_w1(a, b):
             w1_raw[a, b] = held([P, 4, 512], F32, "w1_raw%d%d" % (a, b), tag="slot%d%d" % (a, b))
@@ -90,9 +89,9 @@ def tile_list_weld_pass_scores_kernel(
             )
 
         load_w1(0, 0)
-        load_w1(1, 0)
         load_tab(1)
-        load_dens(0, 0)
+        load_w1(1, 0)
+        load_dens(0, 0, 2)
         load_dens(0, 1)
         load_w1(0, 1)
         load_w1(1, 1)
@@ -150,7 +149,7 @@ def tile_list_weld_pass_scores_kernel(
         tex, lin, h_bf, h_c, h_s = {}, {}, {}, {}, {}
 
         def texture(b, jh):
-            tex[b, jh] = ring.tile([P, 4, HALF], F32, name="tex")
+            tex[b, jh] = ring.tile([P, 4, HALF], F32, name="tex", bufs=3)
             for t in range(4):
                 bank = psum.tile([P, HALF], F32, name="tex_bank", bufs=3)
                 c0 = 512 * b + P * t
@@ -170,7 +169,7 @@ def tile_list_weld_pass_scores_kernel(
             nc.vector.tensor_tensor(tex[b, jh][:, ts, :], tex[b, jh][:, ts, :], dens_sb[b, jh][:, ts, :], ALU.mult)
 
         def linear(b, jh, u):
-            lin[b, jh, u] = psum.tile([P, 4, P], F32, name="lin_bank", bufs=3)
+            lin[b, jh, u] = psum.tile([P, 4, P], F32, name="lin_bank", tag="acc", bufs=5)
             cols = slice(HALF * jh + P * u, HALF * jh + P * (u + 1))
             for t in range(4):
                 for a in range(2):
@@ -221,7 +220,7 @@ def tile_list_weld_pass_scores_kernel(
         def scores(mt, jh):
             if jh == 0:
                 e_sb[mt] = held([P, S], F32, "e%d" % mt, tag="slot%d%d" % (mt % 2, mt // 2))
-            bank = psum.tile([P, HALF], F32, name="e_bank", bufs=2)
+            bank = psum.tile([P, HALF], F32, name="e_bank", tag="acc", bufs=5)
             cols = slice(P * (mt % 2), P * (mt % 2 + 1))
             for b in range(2):
                 nc.tensor.matmul_mx(
@@ -250,16 +249,21 @@ def tile_list_weld_pass_scores_kernel(
             w2_p[:].rearrange("p a (b t m) -> p (a b) t m", t=4, m=P),
             w2_s[:].rearrange("p a (b m t) -> p (a b) t m", t=4, m=P),
         )
-        for a in range(2):
-            cast_w1(a, 0, nc.vector.tensor_copy, 1)
-        for a in range(2):
-            quant_w1(a, 0)
+        cast_w1(0, 0, nc.scalar.copy, 1)
+        quant_w1(0, 0)
         for jh in range(2):
             gather_v_words(1, HALF * jh, HALF * (jh + 1))
-
         texture(0, 0)
+        cast_w1(1, 0, nc.vector.tensor_copy, 1)
+        weigh(0, 0, slice(0, 1))
+        quant_w1(1, 0)
+        for u in range(4):
+            linear(0, 0, u)
         texture(0, 1)
-        chunk(0, 0, 1, lambda: None)
+        for t in range(1, 4):
+            weigh(0, 0, slice(t, t + 1))
+        for u in range(4):
+            combine(0, 0, u)
         texture(1, 0)
         for a in range(2):
             cast_w1(a, 1, nc.scalar.copy, 2)
@@ -299,7 +303,7 @@ def tile_list_weld_pass_scores_kernel(
             nc.vector.tensor_tensor(diff[mt][:], e_sb[mt][:].indirect(pos2_sb[:]), root[mt][:], ALU.subtract)
 
         def finish(mt):
-            res = ring.tile([P, NP], F32, name="res", bufs=4)
+            res = ring.tile([P, NP], F32, name="res", bufs=3)
             nc.vector.scalar_tensor_tensor(res[:], diff[mt][:], -1.0, wgt[mt][:], ALU.mult, ALU.mult)
             nc.sync.dma_start(out[P * mt : P * (mt + 1), :], res[:])
 

@@ -65,13 +65,6 @@ def tile_list_weld_pass_scores_kernel(
         def load_tab(a):
             nc.sync.dma_start(tab_w[a][:], tab_words[a].rearrange("p t i -> p (t i)").bitcast(I32))
 
-        load_tab(0)
-        for q in (0, 2, 1, 3):
-            nc.sync.dma_start(
-                w2_s[32 * q : 32 * q + 4, :, :].bitcast(I32),
-                w2_scales[:, 4 * q : 4 * q + 4, :].rearrange("a r t -> r a t").bitcast(I32),
-            )
-
         dens_sb = {}
         w1_raw = {}
 
@@ -88,12 +81,18 @@ def tile_list_weld_pass_scores_kernel(
                 w1[512 * a : 512 * (a + 1), 512 * b : 512 * (b + 1)].rearrange("(p i) c -> p i c", i=4),
             )
 
+        for q in (0, 2, 1, 3):
+            nc.sync.dma_start(
+                w2_s[32 * q : 32 * q + 4, :, :].bitcast(I32),
+                w2_scales[:, 4 * q : 4 * q + 4, :].rearrange("a r t -> r a t").bitcast(I32),
+            )
         load_w1(0, 0)
+        load_tab(0)
         load_tab(1)
         load_w1(1, 0)
         load_dens(0, 0, 2)
-        load_dens(0, 1)
         load_w1(0, 1)
+        load_dens(0, 1)
         load_w1(1, 1)
         load_dens(1, 0)
         load_dens(1, 1)
@@ -244,12 +243,12 @@ def tile_list_weld_pass_scores_kernel(
 
         for a in range(2):
             gather_v_scales(a)
-        gather_v_words(0, 0, S)
         nc.vector.tensor_copy(
             w2_p[:].rearrange("p a (b t m) -> p (a b) t m", t=4, m=P),
             w2_s[:].rearrange("p a (b m t) -> p (a b) t m", t=4, m=P),
         )
         cast_w1(0, 0, nc.scalar.copy, 1)
+        gather_v_words(0, 0, S)
         quant_w1(0, 0)
         for jh in range(2):
             gather_v_words(1, HALF * jh, HALF * (jh + 1))

from contextlib import ExitStack

import concourse.mybir as mybir

K, T, S, H, T3, S2, NP = 1024, 4096, 1024, 1024, 2048, 512, 512
FLOPS = 2 * (2 * K * H * S + H * S2 * S)

F32 = mybir.dt.float32
BF16 = mybir.dt.bfloat16
I32 = mybir.dt.int32
U32 = mybir.dt.uint32
U16 = mybir.dt.uint16
U8 = mybir.dt.uint8
FP8X4 = mybir.dt.float8_e4m3fn_x4
FP4X4 = mybir.dt.float4_e2m1fn_x4
ALU = mybir.AluOpType
ACT = mybir.ActivationFunctionType

P = 128
HALF = 512


def tile_list_weld_pass_scores_kernel(
    tc, tab_words, tab_scales, offs, tab2_words, tab2_scales, offs2, pos1, pos2, w1, w2_words, w2_scales, dens, sharp, out
):
    nc = tc.nc
    with ExitStack() as ctx:
        lists = ctx.enter_context(tc.tile_pool(name="lists", bufs=1))
        keep = ctx.enter_context(tc.tile_pool(name="keep", bufs=1))
        ring = ctx.enter_context(tc.tile_pool(name="ring", bufs=2))
        psum = ctx.enter_context(tc.psum_pool(name="psum", bufs=1))

        def held(shape, dtype, name, tag=""):
            return keep.tile(shape, dtype, name=name, tag=tag, align_bytes=64)

        offs_sb = lists.tile([P, S // 16], U16, name="offs_sb")
        offs2_sb = lists.tile([P, S2 // 16], U16, name="offs2_sb")
        pos1_sb = lists.tile([P, NP // 16], U16, name="pos1_sb")
        pos2_sb = lists.tile([P, NP // 16], U16, name="pos2_sb")

        tab_s = held([P, 2, T], U8, "tab_s")
        w2_s = held([P, 2, H], U8, "w2_s")
        tab2_s = held([P, T3], U8, "tab2_s")
        w2_w = held([P, 2, 2 * H], U8, "w2_w")
        tab_w = [held([P, T], I32, "tab_w%d" % a) for a in range(2)]
        tab2_w = [held([P, T3], I32, "tab2_w%d" % a) for a in range(2)]
        sharp_sb = held([P, 4], F32, "sharp_sb")

        nc.gpsimd.memset(tab_s[:, 0, :].bitcast(I32), 0)
        nc.vector.memset(tab_s[:, 1, :].bitcast(I32), 0)
        nc.vector.memset(w2_s[:].rearrange("p a t -> p (a t)").bitcast(I32), 0)
        nc.gpsimd.memset(tab2_s[:].bitcast(I32), 0)

        nc.sync.dma_start(offs_sb[:], offs)
        nc.sync.dma_start(offs2_sb[:], offs2)
        nc.sync.dma_start(pos1_sb[:], pos1)
        nc.sync.dma_start(pos2_sb[:], pos2)
        nc.sync.dma_start(w2_w[:].bitcast(I32), w2_words.rearrange("a p c -> p a c").bitcast(I32))
        for q in (0, 2, 1, 3):
            nc.sync.dma_start(
                tab_s[32 * q : 32 * q + 4, :, :].bitcast(I32),
                tab_scales[:, 4 * q : 4 * q + 4, :].rearrange("a r t -> r a t").bitcast(I32),
            )

        def load_tab(a):
            nc.sync.dma_start(tab_w[a][:], tab_words[a].rearrange("p t i -> p (t i)").bitcast(I32))

        dens_sb = {}
        w1_raw = {}

        def load_dens(b, jh, step=4):
            dens_sb[b, jh] = held([P, 4, HALF], F32, "dens%d%d" % (b, jh))
            rows = dens[512 * b : 512 * (b + 1), HALF * jh : HALF * (jh + 1)].rearrange("(p t) j -> p t j", t=4)
            for t in range(0, 4, step):
                nc.sync.dma_start(dens_sb[b, jh][:, t : t + step, :], rows[:, t : t + step, :])

        def load_w1(a, b):
            w1_raw[a, b] = held([P, 4, 512], F32, "w1_raw%d%d" % (a, b), tag="slot%d%d" % (a, b))
            nc.sync.dma_start(
                w1_raw[a, b][:],
                w1[512 * a : 512 * (a + 1), 512 * b : 512 * (b + 1)].rearrange("(p i) c -> p i c", i=4),
            )

        for q in (0, 2, 1, 3):
            nc.sync.dma_start(
                w2_s[32 * q : 32 * q + 4, :, :].bitcast(I32),
                w2_scales[:, 4 * q : 4 * q + 4, :].rearrange("a r t -> r a t").bitcast(I32),
            )
        load_w1(0, 0)
        load_tab(0)
        load_tab(1)
        load_w1(1, 0)
        load_dens(0, 0, 2)
        load_w1(0, 1)
        load_dens(0, 1)
        load_w1(1, 1)
        load_dens(1, 0)
        load_dens(1, 1)
        for q in (0, 2, 1, 3):
            nc.sync.dma_start(
                tab2_s[32 * q : 32 * q + 8, :].bitcast(I32),
                tab2_scales[:, 4 * q : 4 * q + 4, :].bitcast(I32),
            )
        for a in range(2):
            nc.sync.dma_start(tab2_w[a][:], tab2_words[a].rearrange("p t i -> p (t i)").bitcast(I32))
        with nc.allow_non_contiguous_dma("one factor a partition"):
            nc.sync.dma_start(sharp_sb[:], sharp.rearrange("(c p) -> p c", p=P))

        w2_c = held([P, 2, 2 * H], U8, "w2_c")
        w2_p = held([P, 2, H], U8, "w2_p")
        nc.vector.tensor_copy(
            w2_c[:].rearrange("p a c -> p (a c)").bitcast(U16).rearrange("p (g t m) -> p g t m", t=4, m=P),
            w2_w[:].rearrange("p a c -> p (a c)").bitcast(U16).rearrange("p (g m t) -> p g t m", t=4, m=P),
        )

        v_w, v_s = {}, {}

        for a in range(2):
            v_w[a] = held([P, S], U32, "v_w%d" % a)
            v_s[a] = held([P, S], U8, "v_s%d" % a)

        def gather_v_words(a, j0, j1):
            nc.vector.tensor_copy(v_w[a][:, j0:j1], tab_w[a][:].bitcast(U32).indirect(offs_sb[:, j0 // 16 : j1 // 16]))

        def gather_v_scales(a):
            nc.vector.tensor_copy(v_s[a][:], tab_s[:, a, :].indirect(offs_sb[:]))

        w1_bf, w1_c, w1_s = {}, {}, {}

        def cast_w1(a, b, copy, parts):
            w1_bf[a, b] = ring.tile([P, 4, P, 4], BF16, name="w1_bf", align_bytes=64)
            for m0 in range(0, P, P // parts):
                ms = slice(m0, m0 + P // parts)
                copy(
                    w1_bf[a, b][:].rearrange("p t m i -> p m t i")[:, ms],
                    w1_raw[a, b][:].rearrange("p i (m t) -> p m t i", t=4)[:, ms],
                )

        def quant_w1(a, b):
            w1_c[a, b] = held([P, 512], U32, "w1_c%d%d" % (a, b))
            w1_s[a, b] = held([P, 512], U8, "w1_s%d%d" % (a, b))
            nc.vector.quantize_mx(
                out=w1_c[a, b][:].bitcast(FP8X4),
                scales=w1_s[a, b][:],
                in_=w1_bf[a, b][:].rearrange("p t m i -> p (t m i)"),
            )

        tex, lin, h_bf, h_c, h_s = {}, {}, {}, {}, {}

        def texture(b, jh):
            tex[b, jh] = ring.tile([P, 4, HALF], F32, name="tex", bufs=3)
            for t in range(4):
                bank = psum.tile([P, HALF], F32, name="tex_bank", bufs=3)
                c0 = 512 * b + P * t
                for a in range(2):
                    nc.tensor.matmul_mx(
                        out=bank[:],
                        lhsT=w2_c[:, a, 2 * c0 : 2 * (c0 + P)].bitcast(FP4X4),
                        lhsT_scale=w2_p[:, a, c0 : c0 + P],
                        rhs=v_w[a][:, HALF * jh : HALF * (jh + 1)].bitcast(FP8X4),
                        rhs_scale=v_s[a][:, HALF * jh : HALF * (jh + 1)],
                        start=(a == 0),
                        stop=(a == 1),
                    )
                nc.scalar.activation(tex[b, jh][:, t, :], bank[:], ACT.Tanh)

        def weigh(b, jh, ts):
            nc.vector.tensor_tensor(tex[b, jh][:, ts, :], tex[b, jh][:, ts, :], dens_sb[b, jh][:, ts, :], ALU.mult)

        def linear(b, jh, u):
            lin[b, jh, u] = psum.tile([P, 4, P], F32, name="lin_bank", tag="acc", bufs=5)
            cols = slice(HALF * jh + P * u, HALF * jh + P * (u + 1))
            for t in range(4):
                for a in range(2):
                    nc.tensor.matmul_mx(
                        out=lin[b, jh, u][:, t, :],
                        lhsT=w1_c[a, b][:, P * t : P * (t + 1)].bitcast(FP8X4),
                        lhsT_scale=w1_s[a, b][:, P * t : P * (t + 1)],
                        rhs=v_w[a][:, cols].bitcast(FP8X4),
                        rhs_scale=v_s[a][:, cols],
                        start=(a == 0),
                        stop=(a == 1),
                    )

        def combine(b, jh, u):
            if u == 0:
                h_bf[b, jh] = ring.tile([P, HALF, 4], BF16, name="h_bf", align_bytes=64)
            cols = slice(P * u, P * (u + 1))
            nc.vector.tensor_tensor(
                h_bf[b, jh][:, cols, :].rearrange("p (c i) t -> p c t i", i=2),
                lin[b, jh, u][:].rearrange("p t (c i) -> p c t i", i=2),
                tex[b, jh][:, :, cols].rearrange("p t (c i) -> p c t i", i=2),
                ALU.add,
            )

        def quant_h(b, jh):
            h_c[b, jh] = held([P, HALF], U32, "h_c%d%d" % (b, jh))
            h_s[b, jh] = held([P, HALF], U8, "h_s%d%d" % (b, jh))
            nc.vector.quantize_mx(
                out=h_c[b, jh][:].bitcast(FP8X4),
                scales=h_s[b, jh][:],
                in_=h_bf[b, jh][:].rearrange("p j t -> p (j t)"),
            )

        v2_w, v2_s = {}, {}

        def gather_v2_scales(mh):
            v2_s[mh] = held([P, 256], U8, "v2_s%d" % mh)
            nc.vector.tensor_copy(v2_s[mh][:], tab2_s[:].indirect(offs2_sb[:, 16 * mh : 16 * (mh + 1)]))

        def gather_v2_words(a, mh):
            v2_w[a, mh] = held([P, 256], U32, "v2_w%d%d" % (a, mh))
            nc.vector.tensor_copy(
                v2_w[a, mh][:], tab2_w[a][:].bitcast(U32).indirect(offs2_sb[:, 16 * mh : 16 * (mh + 1)])
            )

        e_sb = {}

        def scores(mt, jh):
            if jh == 0:
                e_sb[mt] = held([P, S], F32, "e%d" % mt, tag="slot%d%d" % (mt % 2, mt // 2))
            bank = psum.tile([P, HALF], F32, name="e_bank", tag="acc", bufs=5)
            cols = slice(P * (mt % 2), P * (mt % 2 + 1))
            for b in range(2):
                nc.tensor.matmul_mx(
                    out=bank[:],
                    lhsT=v2_w[b, mt // 2][:, cols].bitcast(FP8X4),
                    lhsT_scale=v2_s[mt // 2][4 * b :, cols],
                    rhs=h_c[b, jh][:].bitcast(FP8X4),
                    rhs_scale=h_s[b, jh][:],
                    start=(b == 0),
                    stop=(b == 1),
                )
            nc.scalar.copy(e_sb[mt][:, HALF * jh : HALF * (jh + 1)], bank[:])

        def chunk(b, jh, step, before_combine):
            for t in range(0, 4, step):
                weigh(b, jh, slice(t, t + step))
            before_combine()
            for u in range(4):
                linear(b, jh, u)
                combine(b, jh, u)

        for a in range(2):
            gather_v_scales(a)
        nc.vector.tensor_copy(
            w2_p[:].rearrange("p a (b t m) -> p (a b) t m", t=4, m=P),
            w2_s[:].rearrange("p a (b m t) -> p (a b) t m", t=4, m=P),
        )
        cast_w1(0, 0, nc.scalar.copy, 1)
        gather_v_words(0, 0, S)
        quant_w1(0, 0)
        for jh in range(2):
            gather_v_words(1, HALF * jh, HALF * (jh + 1))
        texture(0, 0)
        cast_w1(1, 0, nc.vector.tensor_copy, 1)
        weigh(0, 0, slice(0, 1))
        quant_w1(1, 0)
        for u in range(4):
            linear(0, 0, u)
        texture(0, 1)
        for t in range(1, 4):
            weigh(0, 0, slice(t, t + 1))
        for u in range(4):
            combine(0, 0, u)
        texture(1, 0)
        for a in range(2):
            cast_w1(a, 1, nc.scalar.copy, 2)
        chunk(0, 1, 4, lambda: quant_h(0, 0))
        texture(1, 1)

        def before_third():
            quant_h(0, 1)
            for a in range(2):
                quant_w1(a, 1)

        chunk(1, 0, 4, before_third)
        chunk(1, 1, 4, lambda: quant_h(1, 0))
        gather_v2_scales(0)
        for a in range(2):
            gather_v2_words(a, 0)
        quant_h(1, 1)
        gather_v2_scales(1)
        for a in range(2):
            gather_v2_words(a, 1)
        scores(0, 0)
        scores(0, 1)
        for mt in (1, 2, 3):
            for jh in range(2):
                scores(mt, jh)

        root, diff, wgt = {}, {}, {}

        def pick_root(mt):
            root[mt] = ring.tile([P, NP], F32, name="root", bufs=4)
            nc.vector.tensor_copy(root[mt][:], e_sb[mt][:].indirect(pos1_sb[:]))
            wgt[mt] = ring.tile([P, NP], F32, name="wgt", bufs=3)
            nc.scalar.activation(wgt[mt][:], root[mt][:], ACT.Sigmoid, scale=sharp_sb[:, mt : mt + 1])

        def pick_cap(mt):
            diff[mt] = ring.tile([P, NP], F32, name="diff")
            nc.vector.tensor_tensor(diff[mt][:], e_sb[mt][:].indirect(pos2_sb[:]), root[mt][:], ALU.subtract)

        def finish(mt):
            res = ring.tile([P, NP], F32, name="res", bufs=3)
            nc.vector.scalar_tensor_tensor(res[:], diff[mt][:], -1.0, wgt[mt][:], ALU.mult, ALU.mult)
            nc.sync.dma_start(out[P * mt : P * (mt + 1), :], res[:])

        pick_root(0)
        pick_root(1)
        pick_cap(0)
        pick_root(2)
        finish(0)
        pick_cap(1)
        pick_root(3)
        finish(1)
        pick_cap(2)
        pick_cap(3)
        finish(2)
        finish(3)
